import numpy as np
import ml_dtypes

BF16 = ml_dtypes.bfloat16


def bf(x):
    return np.asarray(x, np.float32).astype(BF16)


def f32(x):
    return np.asarray(x, np.float32)


def f64(x):
    return np.asarray(x).astype(np.float64)


def striped(idx):
    return np.tile(idx.reshape(-1, 16).T, (8, 1))


S, K, M, N, D, V = 1024, 128, 128, 384, 3, 128


def gelu_tanh(v):
    return 0.5 * v * (1.0 + np.tanh(np.sqrt(2.0 / np.pi) * (v + 0.044715 * v**3)))


def setup_inputs():
    return {"table": bf(np.random.standard_normal((K, S))), "w": bf(np.random.standard_normal((D, K, M)) / np.sqrt(D * K)), "b": f32(0.5 * np.random.standard_normal((M, 1))), "offs": striped(np.random.permutation(np.tile(np.arange(S), 2))[:N])}


def reference(table, w, b, offs):
    idx = offs[:16].T.reshape(-1)
    x = f64(table)[:, idx]
    y = sum(f64(w)[t].T @ x[:, t * V : (t + 1) * V] for t in range(D))
    return gelu_tanh(y + f64(b))

@@ -1,0 +1,45 @@
+import concourse.mybir as mybir
+
+BF16, F32, U16 = mybir.dt.bfloat16, mybir.dt.float32, mybir.dt.uint16
+GELU_TANH = mybir.ActivationFunctionType.Gelu_apprx_tanh
+
+FEATURES = 128
+NODES = 1024
+RELATIONS = 3
+PICKED = 128
+CHANNELS = 128
+PIECE_COLUMNS = PICKED // 16
+
+FLOPS = 2 * FEATURES * CHANNELS * RELATIONS * PICKED
+
+
+def tile_gather_matmul_kernel(tc, table, w, b, offs, out):
+    nc = tc.nc
+    with (
+        tc.tile_pool(name="held", bufs=1) as held,
+        tc.psum_pool(name="psum", bufs=1) as psum,
+    ):
+        offsets = held.tile([128, RELATIONS * PIECE_COLUMNS], U16, name="offsets")
+        nodes = held.tile([FEATURES, NODES], BF16, name="nodes")
+        weights = held.tile([FEATURES, RELATIONS, CHANNELS], BF16, name="weights")
+        bias = held.tile([CHANNELS, 1], F32, name="bias")
+
+        nc.sync.dma_start(offsets[:], offs)
+        nc.sync.dma_start(nodes[:], table)
+        nc.scalar.dma_start(weights[:], w.rearrange("t k m -> k t m"))
+        nc.scalar.dma_start(bias[:], b)
+
+        y = psum.tile([CHANNELS, PICKED], F32, name="y")
+        for t in range(RELATIONS):
+            piece = offsets[:, t * PIECE_COLUMNS : (t + 1) * PIECE_COLUMNS]
+            nc.tensor.matmul(
+                y[:],
+                weights[:, t, :],
+                nodes[:].indirect(piece),
+                start=(t == 0),
+                stop=(t == RELATIONS - 1),
+            )
+
+        result = held.tile([CHANNELS, PICKED], F32, name="result")
+        nc.scalar.activation(result[:], y[:], GELU_TANH, bias=bias[:])
+        nc.sync.dma_start(out, result[:])

@@ -29,6 +29,10 @@ def tile_gather_matmul_kernel(tc, table, w, b, offs, out):
         nc.scalar.dma_start(weights[:], w.rearrange("t k m -> k t m"))
         nc.scalar.dma_start(bias[:], b)
 
+        warm = held.tile([CHANNELS, 1], F32, name="warm")
+        nc.vector.memset(warm[:], 0.0)
+        nc.scalar.activation(warm[:], warm[:], GELU_TANH)
+
         y = psum.tile([CHANNELS, PICKED], F32, name="y")
         for t in range(RELATIONS):
             piece = offsets[:, t * PIECE_COLUMNS : (t + 1) * PIECE_COLUMNS]

@@ -21,13 +21,16 @@ def tile_gather_matmul_kernel(tc, table, w, b, offs, out):
     ):
         offsets = held.tile([128, RELATIONS * PIECE_COLUMNS], U16, name="offsets")
         nodes = held.tile([FEATURES, NODES], BF16, name="nodes")
-        weights = held.tile([FEATURES, RELATIONS, CHANNELS], BF16, name="weights")
+        first_weights = held.tile([FEATURES, CHANNELS], BF16, name="first_weights")
+        later_weights = held.tile([FEATURES, RELATIONS - 1, CHANNELS], BF16, name="later_weights")
         bias = held.tile([CHANNELS, 1], F32, name="bias")
 
         nc.sync.dma_start(offsets[:], offs)
         nc.sync.dma_start(nodes[:], table)
-        nc.scalar.dma_start(weights[:], w.rearrange("t k m -> k t m"))
+        nc.sync.dma_start(later_weights[:], w[1:RELATIONS].rearrange("t k m -> k t m"))
+        nc.scalar.dma_start(first_weights[:], w[0])
         nc.scalar.dma_start(bias[:], b)
+        weights = [first_weights[:]] + [later_weights[:, t, :] for t in range(RELATIONS - 1)]
 
         warm = held.tile([CHANNELS, 1], F32, name="warm")
         nc.vector.memset(warm[:], 0.0)
@@ -38,7 +41,7 @@ def tile_gather_matmul_kernel(tc, table, w, b, offs, out):
             piece = offsets[:, t * PIECE_COLUMNS : (t + 1) * PIECE_COLUMNS]
             nc.tensor.matmul(
                 y[:],
-                weights[:, t, :],
+                weights[t],
                 nodes[:].indirect(piece),
                 start=(t == 0),
                 stop=(t == RELATIONS - 1),

@@ -9,6 +9,7 @@ RELATIONS = 3
 PICKED = 128
 CHANNELS = 128
 PIECE_COLUMNS = PICKED // 16
+ROW_START = 256
 
 FLOPS = 2 * FEATURES * CHANNELS * RELATIONS * PICKED
 
@@ -19,10 +20,13 @@ def tile_gather_matmul_kernel(tc, table, w, b, offs, out):
         tc.tile_pool(name="held", bufs=1) as held,
         tc.psum_pool(name="psum", bufs=1) as psum,
     ):
+        nodes = held.tile([FEATURES, NODES], BF16, name="nodes", align_bytes=ROW_START)
+        first_weights = held.tile([FEATURES, CHANNELS], BF16, name="first_weights", align_bytes=ROW_START)
+        later_weights = held.tile(
+            [FEATURES, RELATIONS - 1, CHANNELS], BF16, name="later_weights", align_bytes=ROW_START
+        )
+        result = held.tile([CHANNELS, PICKED], F32, name="result", align_bytes=ROW_START)
         offsets = held.tile([128, RELATIONS * PIECE_COLUMNS], U16, name="offsets")
-        nodes = held.tile([FEATURES, NODES], BF16, name="nodes")
-        first_weights = held.tile([FEATURES, CHANNELS], BF16, name="first_weights")
-        later_weights = held.tile([FEATURES, RELATIONS - 1, CHANNELS], BF16, name="later_weights")
         bias = held.tile([CHANNELS, 1], F32, name="bias")
 
         nc.sync.dma_start(offsets[:], offs)
@@ -47,6 +51,5 @@ def tile_gather_matmul_kernel(tc, table, w, b, offs, out):
                 stop=(t == RELATIONS - 1),
             )
 
-        result = held.tile([CHANNELS, PICKED], F32, name="result")
         nc.scalar.activation(result[:], y[:], GELU_TANH, bias=bias[:])
         nc.sync.dma_start(out, result[:])

@@ -21,20 +21,20 @@ def tile_gather_matmul_kernel(tc, table, w, b, offs, out):
         tc.psum_pool(name="psum", bufs=1) as psum,
     ):
         nodes = held.tile([FEATURES, NODES], BF16, name="nodes", align_bytes=ROW_START)
-        first_weights = held.tile([FEATURES, CHANNELS], BF16, name="first_weights", align_bytes=ROW_START)
-        later_weights = held.tile(
-            [FEATURES, RELATIONS - 1, CHANNELS], BF16, name="later_weights", align_bytes=ROW_START
+        early_weights = held.tile(
+            [FEATURES, RELATIONS - 1, CHANNELS], BF16, name="early_weights", align_bytes=ROW_START
         )
+        last_weights = held.tile([FEATURES, CHANNELS], BF16, name="last_weights", align_bytes=ROW_START)
         result = held.tile([CHANNELS, PICKED], F32, name="result", align_bytes=ROW_START)
         offsets = held.tile([128, RELATIONS * PIECE_COLUMNS], U16, name="offsets")
         bias = held.tile([CHANNELS, 1], F32, name="bias")
 
         nc.sync.dma_start(offsets[:], offs)
         nc.sync.dma_start(nodes[:], table)
-        nc.sync.dma_start(later_weights[:], w[1:RELATIONS].rearrange("t k m -> k t m"))
-        nc.scalar.dma_start(first_weights[:], w[0])
+        nc.sync.dma_start(last_weights[:], w[RELATIONS - 1])
+        nc.scalar.dma_start(early_weights[:], w[0 : RELATIONS - 1].rearrange("t k m -> k t m"))
         nc.scalar.dma_start(bias[:], b)
-        weights = [first_weights[:]] + [later_weights[:, t, :] for t in range(RELATIONS - 1)]
+        weights = [early_weights[:, t, :] for t in range(RELATIONS - 1)] + [last_weights[:]]
 
         warm = held.tile([CHANNELS, 1], F32, name="warm")
         nc.vector.memset(warm[:], 0.0)

@@ -21,20 +21,20 @@ def tile_gather_matmul_kernel(tc, table, w, b, offs, out):
         tc.psum_pool(name="psum", bufs=1) as psum,
     ):
         nodes = held.tile([FEATURES, NODES], BF16, name="nodes", align_bytes=ROW_START)
-        early_weights = held.tile(
-            [FEATURES, RELATIONS - 1, CHANNELS], BF16, name="early_weights", align_bytes=ROW_START
+        first_weights = held.tile([FEATURES, CHANNELS], BF16, name="first_weights", align_bytes=ROW_START)
+        later_weights = held.tile(
+            [FEATURES, RELATIONS - 1, CHANNELS], BF16, name="later_weights", align_bytes=ROW_START
         )
-        last_weights = held.tile([FEATURES, CHANNELS], BF16, name="last_weights", align_bytes=ROW_START)
         result = held.tile([CHANNELS, PICKED], F32, name="result", align_bytes=ROW_START)
         offsets = held.tile([128, RELATIONS * PIECE_COLUMNS], U16, name="offsets")
         bias = held.tile([CHANNELS, 1], F32, name="bias")
 
         nc.sync.dma_start(offsets[:], offs)
-        nc.sync.dma_start(nodes[:], table)
-        nc.sync.dma_start(last_weights[:], w[RELATIONS - 1])
-        nc.scalar.dma_start(early_weights[:], w[0 : RELATIONS - 1].rearrange("t k m -> k t m"))
-        nc.scalar.dma_start(bias[:], b)
-        weights = [early_weights[:, t, :] for t in range(RELATIONS - 1)] + [last_weights[:]]
+        nc.scalar.dma_start(nodes[:], table)
+        nc.sync.dma_start(first_weights[:], w[0])
+        nc.scalar.dma_start(later_weights[:], w[1:RELATIONS].rearrange("t k m -> k t m"))
+        nc.sync.dma_start(bias[:], b)
+        weights = [first_weights[:]] + [later_weights[:, t, :] for t in range(RELATIONS - 1)]
 
         warm = held.tile([CHANNELS, 1], F32, name="warm")
         nc.vector.memset(warm[:], 0.0)

import concourse.mybir as mybir

BF16, F32, U16 = mybir.dt.bfloat16, mybir.dt.float32, mybir.dt.uint16
GELU_TANH = mybir.ActivationFunctionType.Gelu_apprx_tanh

FEATURES = 128
NODES = 1024
RELATIONS = 3
PICKED = 128
CHANNELS = 128
PIECE_COLUMNS = PICKED // 16
ROW_START = 256

FLOPS = 2 * FEATURES * CHANNELS * RELATIONS * PICKED


def tile_gather_matmul_kernel(tc, table, w, b, offs, out):
    nc = tc.nc
    with (
        tc.tile_pool(name="held", bufs=1) as held,
        tc.psum_pool(name="psum", bufs=1) as psum,
    ):
        nodes = held.tile([FEATURES, NODES], BF16, name="nodes", align_bytes=ROW_START)
        first_weights = held.tile([FEATURES, CHANNELS], BF16, name="first_weights", align_bytes=ROW_START)
        later_weights = held.tile(
            [FEATURES, RELATIONS - 1, CHANNELS], BF16, name="later_weights", align_bytes=ROW_START
        )
        result = held.tile([CHANNELS, PICKED], F32, name="result", align_bytes=ROW_START)
        offsets = held.tile([128, RELATIONS * PIECE_COLUMNS], U16, name="offsets")
        bias = held.tile([CHANNELS, 1], F32, name="bias")

        nc.sync.dma_start(offsets[:], offs)
        nc.scalar.dma_start(nodes[:], table)
        nc.sync.dma_start(first_weights[:], w[0])
        nc.scalar.dma_start(later_weights[:], w[1:RELATIONS].rearrange("t k m -> k t m"))
        nc.sync.dma_start(bias[:], b)
        weights = [first_weights[:]] + [later_weights[:, t, :] for t in range(RELATIONS - 1)]

        warm = held.tile([CHANNELS, 1], F32, name="warm")
        nc.vector.memset(warm[:], 0.0)
        nc.scalar.activation(warm[:], warm[:], GELU_TANH)

        y = psum.tile([CHANNELS, PICKED], F32, name="y")
        for t in range(RELATIONS):
            piece = offsets[:, t * PIECE_COLUMNS : (t + 1) * PIECE_COLUMNS]
            nc.tensor.matmul(
                y[:],
                weights[t],
                nodes[:].indirect(piece),
                start=(t == 0),
                stop=(t == RELATIONS - 1),
            )

        nc.scalar.activation(result[:], y[:], GELU_TANH, bias=bias[:])
        nc.sync.dma_start(out, result[:])
